import numpy as np
import ml_dtypes


def mxq(x, axis, fmt="e4m3"):
    dtype, down = {"e4m3": (ml_dtypes.float8_e4m3fn, 7), "e5m2": (ml_dtypes.float8_e5m2, 14)}[fmt]
    v = np.moveaxis(np.asarray(x, np.float32).astype(ml_dtypes.bfloat16).astype(np.float64), axis, -1)
    blocks = v.reshape(v.shape[:-1] + (-1, 32))
    amax = np.abs(blocks).max(-1, keepdims=True)
    byte = np.maximum(np.where(amax > 0, np.frexp(amax)[1] - 1 + 127, 0) - down, 1)
    scale = np.exp2(byte - 127.0)
    codes = (blocks / scale).astype(np.float32).astype(dtype).astype(np.float64)
    return np.moveaxis((codes * scale).reshape(v.shape), -1, axis)


WIDE = False


def mx_kscale(k):
    if not WIDE:
        return np.ones(k)
    levels = np.array([10, -10, 5, -5, 0])
    if k % 512:
        return np.exp2(np.random.permutation(np.resize(levels, k // 32))).repeat(32)
    a = np.empty((k // 512, 16))
    for p in range(k // 512):
        a[p, :8] = np.random.permutation(np.resize(levels, 8))
        for g in range(8):
            far = levels[np.abs(levels - a[p, g]) >= 10]
            a[p, g + 8] = far[np.random.randint(len(far))]
    return np.exp2(a.ravel()).repeat(32)


def f64(x):
    return np.asarray(x).astype(np.float64)


def striped(idx):
    return np.tile(np.asarray(idx).reshape(-1, 16).T, (8, 1)).astype(np.uint16)


def unstriped(offs):
    return offs[:16].T.reshape(-1).astype(np.int64)


E2M1 = np.array([0.0, 0.5, 1.0, 1.5, 2.0, 3.0, 4.0, 6.0, -0.0, -0.5, -1.0, -1.5, -2.0, -3.0, -4.0, -6.0])


def pack_weight(w, fmt):
    k, n = w.shape
    w = f64(np.asarray(w, np.float32).astype(ml_dtypes.bfloat16)).reshape(k // 32, 32, n)
    amax = np.abs(w).max(1)
    if fmt == "e4m3":
        byte = np.frexp(amax)[1] - 1 + 127 - 7
    else:
        mant, ex = np.frexp(amax / 6.0)
        byte = np.where(mant > 0.5, ex, ex - 1) + 127
    byte = np.clip(np.where(amax > 0, byte, 1), 1, 254)
    scaled = (w * np.exp2(127.0 - byte)[:, None, :]).reshape(k, n).astype(np.float32)
    by_word = np.ascontiguousarray(scaled.reshape(k // 512, 128, 4, n).transpose(0, 1, 3, 2))
    if fmt == "e4m3":
        words = by_word.astype(ml_dtypes.float8_e4m3fn).view(np.uint8)
    else:
        c = by_word.astype(ml_dtypes.float4_e2m1fn).view(np.uint8) & 0xF
        words = (c[..., 0::2] | (c[..., 1::2] << 4)).reshape(k // 512, 128, 2 * n)
    return np.ascontiguousarray(words), np.ascontiguousarray(byte.astype(np.uint8).reshape(k // 512, 16, n))


def unpack_weight(words, scales, fmt):
    g, _, n = scales.shape
    words = np.ascontiguousarray(words).reshape(g, 128, n, -1)
    if fmt == "e4m3":
        vals = words.view(ml_dtypes.float8_e4m3fn).astype(np.float64)
    else:
        nib = np.empty((g, 128, n, 4), np.uint8)
        nib[..., 0::2] = words & 0xF
        nib[..., 1::2] = words >> 4
        vals = E2M1[nib]
    vals = vals * np.repeat(np.exp2(scales.astype(np.float64) - 127.0), 8, axis=1)[..., None]
    return vals.transpose(0, 1, 3, 2).reshape(g * 512, n)


def sigmoid(v):
    return 1.0 / (1.0 + np.exp(-v))


def bf(x):
    return np.asarray(x, np.float32).astype(ml_dtypes.bfloat16)


def planes(Y):
    r, m = Y.shape
    b = f64(bf(Y)).reshape(r // 32, 32, m)
    amax = np.abs(b).max(1)
    byte = np.clip(np.where(amax > 0, np.frexp(amax)[1] - 1 + 127 - 7, 1), 1, 254)
    codes = (b * np.exp2(127.0 - byte)[:, None, :]).reshape(r, m).astype(np.float32).astype(ml_dtypes.float8_e4m3fn).view(np.uint8)
    words = codes.reshape(r // 512, 128, 4, m).transpose(0, 1, 3, 2)
    return np.ascontiguousarray(words), np.ascontiguousarray(byte.astype(np.uint8).reshape(r // 512, 16, m))


K, I, L, S, T, N, M = 1024, 512, 512, 512, 512, 512, 512


def setup_inputs():
    n = np.random.standard_normal
    idx = np.random.randint(0, I, T)
    idx2 = np.random.randint(0, S, T)
    fk = mx_kscale(K)
    fl = mx_kscale(L)
    fm = mx_kscale(M)
    xap = pack_weight(n((K, I)) / fk[:, None], "e2m1")
    wap = pack_weight(n((K, N)) * 1 / np.sqrt(K) * fk[:, None], "e4m3")
    wbp = pack_weight(n((L, N)) * 1 / np.sqrt(L) * fl[:, None], "e2m1")
    xgp = pack_weight(n((M, T)) / fm[:, None], "e4m3")
    wgp = pack_weight(n((M, N)) * 1 / np.sqrt(M) * fm[:, None], "e2m1")
    return {
        "xa_words": xap[0],
        "xa_scales": xap[1],
        "wa_words": wap[0],
        "wa_scales": wap[1],
        "xb": (n((L, S)) / fl[:, None]).astype(np.float32),
        "wb_words": wbp[0],
        "wb_scales": wbp[1],
        "xg_words": xgp[0],
        "xg_scales": xgp[1],
        "wg_words": wgp[0],
        "wg_scales": wgp[1],
        "offs": striped(idx),
        "offs2": striped(idx2),
    }


def reference(xa_words, xa_scales, wa_words, wa_scales, xb, wb_words, wb_scales, xg_words, xg_scales, wg_words, wg_scales, offs, offs2):
    idx = unstriped(offs)
    idx2 = unstriped(offs2)
    xau = unpack_weight(xa_words, xa_scales, "e2m1")
    wau = unpack_weight(wa_words, wa_scales, "e4m3")
    wbu = unpack_weight(wb_words, wb_scales, "e2m1")
    xgu = unpack_weight(xg_words, xg_scales, "e4m3")
    wgu = unpack_weight(wg_words, wg_scales, "e2m1")
    za = wau.T @ xau
    xbq = mxq(f64(xb), 0, "e4m3")
    zb = wbu.T @ xbq
    g = wgu.T @ xgu
    y = zb[:, idx2] + sigmoid(g) * (za[:, idx] - zb[:, idx2])
    words, scales = planes(y)
    return y, words, scales

@@ -1,0 +1,218 @@
+from contextlib import ExitStack
+
+import concourse.mybir as mybir
+
+F32 = mybir.dt.float32
+BF16 = mybir.dt.bfloat16
+I32 = mybir.dt.int32
+U16 = mybir.dt.uint16
+U8 = mybir.dt.uint8
+FP8X4 = mybir.dt.float8_e4m3fn_x4
+FP4X4 = mybir.dt.float4_e2m1fn_x4
+MULT = mybir.AluOpType.mult
+ADD = mybir.AluOpType.add
+SIGMOID = mybir.ActivationFunctionType.Sigmoid
+
+P = 128
+PACK = 4
+W = 512
+SPARE = 16
+CHUNKS = ((0, 256), (256, 384), (384, 512))
+FLOPS = 2 * 512 * 512 * (1024 + 512 + 512)
+
+
+def tile_moe_combine_gated_by_token_pl_kernel(
+    tc, xa_words, xa_scales, wa_words, wa_scales, xb, wb_words, wb_scales,
+    xg_words, xg_scales, wg_words, wg_scales, offs, offs2, out_0, out_1, out_2,
+):
+    nc = tc.nc
+    with ExitStack() as ctx:
+        keep = ctx.enter_context(tc.tile_pool(name="keep", bufs=1))
+        psum = ctx.enter_context(tc.psum_pool(name="psum", bufs=1))
+
+        def new(name, shape, dtype, tag=None):
+            return keep.tile(shape, dtype, name=name, tag=tag or name, align_bytes=64)
+
+        def load_rows(dst, scales):
+            passes = scales.shape[0]
+            nc.sync.dma_start(
+                out=dst.bitcast(I32).rearrange("q (z c) -> q z c", z=passes),
+                in_=scales.bitcast(I32).rearrange("z q c -> q z c"),
+            )
+
+        def deal(dst, src, passes, run):
+            nc.vector.tensor_copy(
+                out=dst.rearrange("p (j b i) -> p b j i", j=PACK, i=run),
+                in_=src.rearrange("p (b i j) -> p b j i", j=PACK, i=run),
+            )
+
+        rows = new("rows", [16, 7 * W], U8)
+        planes = new("planes", [P, 7 * W], U8)
+        nc.gpsimd.memset(planes[:].bitcast(I32), 0)
+        xg_plane, xa_plane = planes[:, 4 * W : 5 * W], planes[:, 5 * W :]
+        wb_plane = new("wb_plane", [P, W], U8)
+        wg_plane = new("wg_plane", [P, W], U8)
+        wa_plane = new("wa_plane", [P, 2 * W], U8)
+
+        warm_in = new("warm_in", [P, 1], F32)
+        warm_out = new("warm_out", [P, 1], F32)
+        nc.vector.memset(warm_in[:], 0.0)
+        nc.scalar.activation(warm_out[:], warm_in[:], SIGMOID)
+
+        za = [new("za%d" % j, [P, W + SPARE if j < 2 else W], F32) for j in range(PACK)]
+        zb = [new("zb%d" % j, [P, W + SPARE], F32) for j in range(PACK)]
+        for tile in zb + za[:2]:
+            nc.gpsimd.memset(tile[:, W:], 0.0)
+
+        half = W // 2
+        xb_rows = xb.rearrange("(p j) s -> p j s", j=PACK)
+        xb_raw = new("xb_raw", [P, PACK, W], F32)
+        wb_raw = new("wb_raw", [P, 2 * W], U8)
+        load_rows(rows[:, 4 * W : 5 * W], xg_scales)
+        load_rows(rows[:, 5 * W :], xa_scales)
+        load_rows(rows[:, 0:W], wb_scales)
+        load_rows(rows[:, W : 2 * W], wg_scales)
+        load_rows(rows[:, 2 * W : 4 * W], wa_scales)
+        nc.sync.dma_start(out=wb_raw[:].bitcast(I32), in_=wb_words[0].bitcast(I32))
+        wg_raw = new("wg_raw", [P, 2 * W], U8)
+        nc.sync.dma_start(out=wg_raw[:].bitcast(I32), in_=wg_words[0].bitcast(I32))
+        nc.sync.dma_start(out=xb_raw[:], in_=xb_rows)
+        for q in range(4):
+            nc.scalar.dma_start(
+                out=planes[32 * q : 32 * q + 4, :].bitcast(I32), in_=rows[4 * q : 4 * q + 4, :].bitcast(I32)
+            )
+        xg_codes = new("xg_codes", [P, W], I32)
+        nc.sync.dma_start(out=xg_codes[:], in_=xg_words[0].rearrange("p c r -> p (c r)").bitcast(I32))
+        list_b = keep.tile([P, W // 16], U16, name="list_b")
+        nc.sync.dma_start(list_b[:], offs2)
+        list_a = keep.tile([P, W // 16], U16, name="list_a")
+        nc.sync.dma_start(list_a[:], offs)
+
+        wb_codes = new("wb_codes", [P, 2 * W], U8)
+        deal(wb_codes[:].bitcast(U16), wb_raw[:].bitcast(U16), 1, 8)
+        xb_bf = [new("xb_bf%d" % h, [P, half * PACK], BF16) for h in range(2)]
+        xb_codes = [new("xb_codes%d" % h, [P, half], I32) for h in range(2)]
+        xb_plane = [new("xb_plane%d" % h, [P, half], U8) for h in range(2)]
+
+        def weave(engine_copy, dst, src):
+            engine_copy(
+                out=dst.rearrange("p (c i t) -> p c t i", i=4, t=PACK),
+                in_=src.rearrange("p t (c i) -> p c t i", i=4),
+            )
+
+        wg_codes = new("wg_codes", [P, 2 * W], U8)
+        deal(wg_codes[:].bitcast(U16), wg_raw[:].bitcast(U16), 1, 8)
+        wa_raw = new("wa_raw", [P, 2 * W], I32, tag="wb_raw")
+        nc.sync.dma_start(
+            out=wa_raw[:].rearrange("p (z c) -> p z c", z=2),
+            in_=wa_words.rearrange("z p c r -> p z (c r)").bitcast(I32),
+        )
+        xa_codes = new("xa_codes", [P, 2, 2 * W], U8, tag="wg_raw")
+        nc.sync.dma_start(out=xa_codes[:].bitcast(I32), in_=xa_words.rearrange("z p c -> p z c").bitcast(I32))
+        weave(nc.scalar.copy, xb_bf[0][:], xb_raw[:, :, :half])
+        deal(wg_plane[:], planes[:, W : 2 * W], 1, 16)
+        deal(wb_plane[:], planes[:, 0:W], 1, 16)
+        weave(nc.vector.tensor_copy, xb_bf[1][:], xb_raw[:, :, half:])
+        for h in (1, 0):
+            nc.vector.quantize_mx(out=xb_codes[h][:].bitcast(FP8X4), scales=xb_plane[h][:], in_=xb_bf[h][:])
+        wa_codes = new("wa_codes", [P, 2 * W], I32)
+        deal(wa_plane[:], planes[:, 2 * W : 4 * W], 2, 16)
+        deal(wa_codes[:], wa_raw[:], 2, 4)
+
+        gate_b = [new("gate_b%d" % j, [P, W], F32) for j in range(PACK)]
+        gate_a = [new("gate_a%d" % j, [P, W], F32) for j in range(PACK)]
+        part_b = new("part_b", [P, PACK, W], F32)
+        g_banks = []
+        for j in range(PACK):
+            g_bank = psum.tile([P, W], F32, name="g_bank%d" % j)
+            nc.tensor.matmul_mx(
+                out=g_bank[:],
+                lhsT=wg_codes[:, 2 * P * j : 2 * P * (j + 1)].bitcast(FP4X4),
+                lhsT_scale=wg_plane[:, P * j : P * (j + 1)],
+                rhs=xg_codes[:].bitcast(FP8X4),
+                rhs_scale=xg_plane,
+                start=True, stop=True,
+            )
+            nc.scalar.activation(gate_b[j][:], g_bank[:], SIGMOID, scale=-1.0)
+            bank = psum.tile([P, W], F32, name="z_bank%d" % j, tag="z_bank%d" % j)
+            for h in (1, 0):
+                nc.tensor.matmul_mx(
+                    out=bank[:, h * half : (h + 1) * half],
+                    lhsT=wb_codes[:, 2 * P * j : 2 * P * (j + 1)].bitcast(FP4X4),
+                    lhsT_scale=wb_plane[:, P * j : P * (j + 1)],
+                    rhs=xb_codes[h][:].bitcast(FP8X4),
+                    rhs_scale=xb_plane[h][:],
+                    start=True, stop=True,
+                )
+            g_banks.append(g_bank)
+            nc.scalar.copy(zb[j][:, :W], bank[:])
+            nc.vector.tensor_tensor(part_b[:, j, :], zb[j][:].indirect(list_b[:]), gate_b[j][:], MULT)
+
+        for j in range(PACK):
+            bank = psum.tile([P, W], F32, name="za_bank%d" % j, tag="z_bank%d" % j)
+            for z in range(2):
+                cols = slice(2 * P * j + P * z, 2 * P * j + P * (z + 1))
+                nc.tensor.matmul_mx(
+                    out=bank[:],
+                    lhsT=wa_codes[:, cols].bitcast(FP8X4),
+                    lhsT_scale=wa_plane[:, cols],
+                    rhs=xa_codes[:, z, :].bitcast(FP4X4),
+                    rhs_scale=xa_plane[:, z * W : (z + 1) * W],
+                    start=(z == 0), stop=(z == 1),
+                )
+            nc.scalar.copy(za[j][:, :W], bank[:])
+            nc.scalar.activation(gate_a[j][:], g_banks[j][:], SIGMOID)
+
+        part_a = new("part_a", [P, PACK, W], F32)
+        for j in range(2):
+            nc.vector.tensor_tensor(part_a[:, j, :], za[j][:].indirect(list_a[:]), gate_a[j][:], MULT)
+
+        y_rows = out_0.rearrange("(p j) t -> p j t", j=PACK)
+        words_out = out_1[0].rearrange("p c r -> p (c r)").bitcast(I32)
+        y_plane = new("y_plane", [P, W], U8)
+
+        def gather(c, j):
+            t0, t1 = CHUNKS[c]
+            nc.vector.tensor_tensor(
+                part_a[:, j, t0:t1], za[j][:].indirect(list_a[:, t0 // 16 : t1 // 16]), gate_a[j][:, t0:t1], MULT
+            )
+
+        ys = {}
+        ybf = {}
+
+        def add(c):
+            t0, t1 = CHUNKS[c]
+            ys[c] = new("y%d" % c, [P, PACK, t1 - t0], F32)
+            nc.vector.tensor_tensor(ys[c][:], part_a[:, :, t0:t1], part_b[:, :, t0:t1], ADD)
+            nc.sync.dma_start(out=y_rows[:, :, t0:t1], in_=ys[c][:])
+
+        def round_(c, engine_copy):
+            t0, t1 = CHUNKS[c]
+            ybf[c] = new("ybf%d" % c, [P, (t1 - t0) * PACK], BF16)
+            weave(engine_copy, ybf[c][:], ys[c][:])
+
+        def quant(c):
+            t0, t1 = CHUNKS[c]
+            codes = new("y_codes%d" % c, [P, t1 - t0], I32)
+            nc.vector.quantize_mx(out=codes[:].bitcast(FP8X4), scales=y_plane[:, t0:t1], in_=ybf[c][:])
+            nc.sync.dma_start(out=words_out[:, t0:t1], in_=codes[:])
+
+        gather(0, 2)
+        gather(0, 3)
+        gather(1, 2)
+        add(0)
+        round_(0, nc.scalar.copy)
+        gather(1, 3)
+        gather(2, 2)
+        add(1)
+        round_(1, nc.scalar.copy)
+        gather(2, 3)
+        quant(0)
+        add(2)
+        quant(1)
+        round_(2, nc.vector.tensor_copy)
+        quant(2)
+        for q in range(4):
+            nc.scalar.dma_start(
+                out=out_2[0, 4 * q : 4 * q + 4, :].bitcast(I32), in_=y_plane[32 * q : 32 * q + 4, :].bitcast(I32)
+            )

@@ -5,6 +5,7 @@ import concourse.mybir as mybir
 F32 = mybir.dt.float32
 BF16 = mybir.dt.bfloat16
 I32 = mybir.dt.int32
+U32 = mybir.dt.uint32
 U16 = mybir.dt.uint16
 U8 = mybir.dt.uint8
 FP8X4 = mybir.dt.float8_e4m3fn_x4
@@ -33,9 +34,9 @@ def tile_moe_combine_gated_by_token_pl_kernel(
         def new(name, shape, dtype, tag=None):
             return keep.tile(shape, dtype, name=name, tag=tag or name, align_bytes=64)
 
-        def load_rows(dst, scales):
+        def load_rows(queue, dst, scales):
             passes = scales.shape[0]
-            nc.sync.dma_start(
+            queue.dma_start(
                 out=dst.bitcast(I32).rearrange("q (z c) -> q z c", z=passes),
                 in_=scales.bitcast(I32).rearrange("z q c -> q z c"),
             )
@@ -48,19 +49,14 @@ def tile_moe_combine_gated_by_token_pl_kernel(
 
         rows = new("rows", [16, 7 * W], U8)
         planes = new("planes", [P, 7 * W], U8)
-        nc.gpsimd.memset(planes[:].bitcast(I32), 0)
+        nc.vector.memset(planes[:].bitcast(I32), 0)
         xg_plane, xa_plane = planes[:, 4 * W : 5 * W], planes[:, 5 * W :]
         wb_plane = new("wb_plane", [P, W], U8)
         wg_plane = new("wg_plane", [P, W], U8)
         wa_plane = new("wa_plane", [P, 2 * W], U8)
 
-        warm_in = new("warm_in", [P, 1], F32)
-        warm_out = new("warm_out", [P, 1], F32)
-        nc.vector.memset(warm_in[:], 0.0)
-        nc.scalar.activation(warm_out[:], warm_in[:], SIGMOID)
-
         za = [new("za%d" % j, [P, W + SPARE if j < 2 else W], F32) for j in range(PACK)]
-        zb = [new("zb%d" % j, [P, W + SPARE], F32) for j in range(PACK)]
+        zb = [new("zb%d" % j, [P, W + SPARE], F32) for j in range(2)]
         for tile in zb + za[:2]:
             nc.gpsimd.memset(tile[:, W:], 0.0)
 
@@ -68,11 +64,11 @@ def tile_moe_combine_gated_by_token_pl_kernel(
         xb_rows = xb.rearrange("(p j) s -> p j s", j=PACK)
         xb_raw = new("xb_raw", [P, PACK, W], F32)
         wb_raw = new("wb_raw", [P, 2 * W], U8)
-        load_rows(rows[:, 4 * W : 5 * W], xg_scales)
-        load_rows(rows[:, 5 * W :], xa_scales)
-        load_rows(rows[:, 0:W], wb_scales)
-        load_rows(rows[:, W : 2 * W], wg_scales)
-        load_rows(rows[:, 2 * W : 4 * W], wa_scales)
+        load_rows(nc.scalar, rows[:, 0:W], wb_scales)
+        load_rows(nc.scalar, rows[:, W : 2 * W], wg_scales)
+        load_rows(nc.sync, rows[:, 2 * W : 4 * W], wa_scales)
+        load_rows(nc.sync, rows[:, 4 * W : 5 * W], xg_scales)
+        load_rows(nc.sync, rows[:, 5 * W :], xa_scales)
         nc.sync.dma_start(out=wb_raw[:].bitcast(I32), in_=wb_words[0].bitcast(I32))
         wg_raw = new("wg_raw", [P, 2 * W], U8)
         nc.sync.dma_start(out=wg_raw[:].bitcast(I32), in_=wg_words[0].bitcast(I32))
@@ -81,6 +77,8 @@ def tile_moe_combine_gated_by_token_pl_kernel(
             nc.scalar.dma_start(
                 out=planes[32 * q : 32 * q + 4, :].bitcast(I32), in_=rows[4 * q : 4 * q + 4, :].bitcast(I32)
             )
+        warm_out = new("warm_out", [16, 1], F32)
+        nc.scalar.activation(warm_out[:], rows[:, 5 * W : 5 * W + 4].bitcast(U32), SIGMOID)
         xg_codes = new("xg_codes", [P, W], I32)
         nc.sync.dma_start(out=xg_codes[:], in_=xg_words[0].rearrange("p c r -> p (c r)").bitcast(I32))
         list_b = keep.tile([P, W // 16], U16, name="list_b")
@@ -102,29 +100,27 @@ def tile_moe_combine_gated_by_token_pl_kernel(
 
         wg_codes = new("wg_codes", [P, 2 * W], U8)
         deal(wg_codes[:].bitcast(U16), wg_raw[:].bitcast(U16), 1, 8)
-        wa_raw = new("wa_raw", [P, 2 * W], I32, tag="wb_raw")
+        wa_raw = new("wa_raw", [P, 2 * W], I32, tag="wg_raw")
         nc.sync.dma_start(
             out=wa_raw[:].rearrange("p (z c) -> p z c", z=2),
             in_=wa_words.rearrange("z p c r -> p z (c r)").bitcast(I32),
         )
-        xa_codes = new("xa_codes", [P, 2, 2 * W], U8, tag="wg_raw")
-        nc.sync.dma_start(out=xa_codes[:].bitcast(I32), in_=xa_words.rearrange("z p c -> p z c").bitcast(I32))
         weave(nc.scalar.copy, xb_bf[0][:], xb_raw[:, :, :half])
+        weave(nc.vector.tensor_copy, xb_bf[1][:], xb_raw[:, :, half:])
+        xa_codes = new("xa_codes", [P, 2, 2 * W], U8, tag="xb_raw")
+        nc.sync.dma_start(out=xa_codes[:].bitcast(I32), in_=xa_words.rearrange("z p c -> p z c").bitcast(I32))
+        nc.vector.quantize_mx(out=xb_codes[1][:].bitcast(FP8X4), scales=xb_plane[1][:], in_=xb_bf[1][:])
         deal(wg_plane[:], planes[:, W : 2 * W], 1, 16)
         deal(wb_plane[:], planes[:, 0:W], 1, 16)
-        weave(nc.vector.tensor_copy, xb_bf[1][:], xb_raw[:, :, half:])
-        for h in (1, 0):
-            nc.vector.quantize_mx(out=xb_codes[h][:].bitcast(FP8X4), scales=xb_plane[h][:], in_=xb_bf[h][:])
-        wa_codes = new("wa_codes", [P, 2 * W], I32)
+        nc.vector.quantize_mx(out=xb_codes[0][:].bitcast(FP8X4), scales=xb_plane[0][:], in_=xb_bf[0][:])
         deal(wa_plane[:], planes[:, 2 * W : 4 * W], 2, 16)
-        deal(wa_codes[:], wa_raw[:], 2, 4)
 
         gate_b = [new("gate_b%d" % j, [P, W], F32) for j in range(PACK)]
-        gate_a = [new("gate_a%d" % j, [P, W], F32) for j in range(PACK)]
+        gate_a = gate_b[1:] + [new("gate_a3", [P, W], F32)]
         part_b = new("part_b", [P, PACK, W], F32)
         g_banks = []
         for j in range(PACK):
-            g_bank = psum.tile([P, W], F32, name="g_bank%d" % j)
+            g_bank = psum.tile([P, W], F32, name="g_bank%d" % j, tag="bank%d" % j)
             nc.tensor.matmul_mx(
                 out=g_bank[:],
                 lhsT=wg_codes[:, 2 * P * j : 2 * P * (j + 1)].bitcast(FP4X4),
@@ -134,7 +130,7 @@ def tile_moe_combine_gated_by_token_pl_kernel(
                 start=True, stop=True,
             )
             nc.scalar.activation(gate_b[j][:], g_bank[:], SIGMOID, scale=-1.0)
-            bank = psum.tile([P, W], F32, name="z_bank%d" % j, tag="z_bank%d" % j)
+            bank = psum.tile([P, W], F32, name="zb_bank%d" % j, tag="bank%d" % (j + 1))
             for h in (1, 0):
                 nc.tensor.matmul_mx(
                     out=bank[:, h * half : (h + 1) * half],
@@ -145,11 +141,14 @@ def tile_moe_combine_gated_by_token_pl_kernel(
                     start=True, stop=True,
                 )
             g_banks.append(g_bank)
-            nc.scalar.copy(zb[j][:, :W], bank[:])
-            nc.vector.tensor_tensor(part_b[:, j, :], zb[j][:].indirect(list_b[:]), gate_b[j][:], MULT)
+            nc.scalar.copy(zb[j % 2][:, :W], bank[:])
+            nc.vector.tensor_tensor(part_b[:, j, :], zb[j % 2][:].indirect(list_b[:]), gate_b[j][:], MULT)
+            if j == 0:
+                wa_codes = new("wa_codes", [P, 2 * W], I32, tag="gate_b0")
+                deal(wa_codes[:], wa_raw[:], 2, 4)
 
         for j in range(PACK):
-            bank = psum.tile([P, W], F32, name="za_bank%d" % j, tag="z_bank%d" % j)
+            bank = psum.tile([P, W], F32, name="za_bank%d" % j, tag="bank%d" % (PACK + (j + 1) % PACK))
             for z in range(2):
                 cols = slice(2 * P * j + P * z, 2 * P * j + P * (z + 1))
                 nc.tensor.matmul_mx(
@@ -161,7 +160,10 @@ def tile_moe_combine_gated_by_token_pl_kernel(
                     start=(z == 0), stop=(z == 1),
                 )
             nc.scalar.copy(za[j][:, :W], bank[:])
-            nc.scalar.activation(gate_a[j][:], g_banks[j][:], SIGMOID)
+            first = W if j < 2 else half
+            nc.scalar.activation(gate_a[j][:, :first], g_banks[j][:, :first], SIGMOID)
+        for j in (2, 3):
+            nc.scalar.activation(gate_a[j][:, half:], g_banks[j][:, half:], SIGMOID)
 
         part_a = new("part_a", [P, PACK, W], F32)
         for j in range(2):
@@ -191,11 +193,11 @@ def tile_moe_combine_gated_by_token_pl_kernel(
             ybf[c] = new("ybf%d" % c, [P, (t1 - t0) * PACK], BF16)
             weave(engine_copy, ybf[c][:], ys[c][:])
 
+        y_codes = new("y_codes", [P, W], I32)
+
         def quant(c):
             t0, t1 = CHUNKS[c]
-            codes = new("y_codes%d" % c, [P, t1 - t0], I32)
-            nc.vector.quantize_mx(out=codes[:].bitcast(FP8X4), scales=y_plane[:, t0:t1], in_=ybf[c][:])
-            nc.sync.dma_start(out=words_out[:, t0:t1], in_=codes[:])
+            nc.vector.quantize_mx(out=y_codes[:, t0:t1].bitcast(FP8X4), scales=y_plane[:, t0:t1], in_=ybf[c][:])
 
         gather(0, 2)
         gather(0, 3)
@@ -208,10 +210,12 @@ def tile_moe_combine_gated_by_token_pl_kernel(
         round_(1, nc.scalar.copy)
         gather(2, 3)
         quant(0)
+        nc.sync.dma_start(out=words_out[:, :half], in_=y_codes[:, :half])
         add(2)
         quant(1)
         round_(2, nc.vector.tensor_copy)
         quant(2)
+        nc.sync.dma_start(out=words_out[:, half:], in_=y_codes[:, half:])
         for q in range(4):
             nc.scalar.dma_start(
                 out=out_2[0, 4 * q : 4 * q + 4, :].bitcast(I32), in_=y_plane[32 * q : 32 * q + 4, :].bitcast(I32)

@@ -5,7 +5,6 @@ import concourse.mybir as mybir
 F32 = mybir.dt.float32
 BF16 = mybir.dt.bfloat16
 I32 = mybir.dt.int32
-U32 = mybir.dt.uint32
 U16 = mybir.dt.uint16
 U8 = mybir.dt.uint8
 FP8X4 = mybir.dt.float8_e4m3fn_x4
@@ -47,16 +46,20 @@ def tile_moe_combine_gated_by_token_pl_kernel(
                 in_=src.rearrange("p (b i j) -> p b j i", j=PACK, i=run),
             )
 
-        rows = new("rows", [16, 7 * W], U8)
+        warm_in = new("warm_in", [P, 1], F32)
+        warm_out = new("warm_out", [P, 1], F32)
+        nc.vector.memset(warm_in[:], 0.0)
+        nc.scalar.activation(warm_out[:], warm_in[:], SIGMOID)
+        rows_raw = new("rows_raw", [P, 2 * W], U8)
+        rows = new("rows", [P, 7 * W], U8)
         planes = new("planes", [P, 7 * W], U8)
-        nc.vector.memset(planes[:].bitcast(I32), 0)
+        nc.gpsimd.memset(planes[:].bitcast(I32), 0)
         xg_plane, xa_plane = planes[:, 4 * W : 5 * W], planes[:, 5 * W :]
-        wb_plane = new("wb_plane", [P, W], U8)
-        wg_plane = new("wg_plane", [P, W], U8)
+        wb_plane, wg_plane = planes[:, :W], planes[:, W : 2 * W]
         wa_plane = new("wa_plane", [P, 2 * W], U8)
 
         za = [new("za%d" % j, [P, W + SPARE if j < 2 else W], F32) for j in range(PACK)]
-        zb = [new("zb%d" % j, [P, W + SPARE], F32) for j in range(2)]
+        zb = [new("zb%d" % j, [P, W + SPARE], F32) for j in range(PACK)]
         for tile in zb + za[:2]:
             nc.gpsimd.memset(tile[:, W:], 0.0)
 
@@ -64,21 +67,26 @@ def tile_moe_combine_gated_by_token_pl_kernel(
         xb_rows = xb.rearrange("(p j) s -> p j s", j=PACK)
         xb_raw = new("xb_raw", [P, PACK, W], F32)
         wb_raw = new("wb_raw", [P, 2 * W], U8)
-        load_rows(nc.scalar, rows[:, 0:W], wb_scales)
-        load_rows(nc.scalar, rows[:, W : 2 * W], wg_scales)
-        load_rows(nc.sync, rows[:, 2 * W : 4 * W], wa_scales)
-        load_rows(nc.sync, rows[:, 4 * W : 5 * W], xg_scales)
-        load_rows(nc.sync, rows[:, 5 * W :], xa_scales)
+        for slot, scales in enumerate((wb_scales, wg_scales)):
+            nc.sync.dma_start(
+                out=rows_raw[:, slot * W : (slot + 1) * W].bitcast(I32),
+                in_=scales.bitcast(I32).broadcast_to([P // 16, 16, W // 4]),
+            )
+        load_rows(nc.sync, rows[:16, 2 * W : 4 * W], wa_scales)
+        load_rows(nc.sync, rows[:16, 4 * W : 5 * W], xg_scales)
+        load_rows(nc.sync, rows[:16, 5 * W :], xa_scales)
         nc.sync.dma_start(out=wb_raw[:].bitcast(I32), in_=wb_words[0].bitcast(I32))
         wg_raw = new("wg_raw", [P, 2 * W], U8)
         nc.sync.dma_start(out=wg_raw[:].bitcast(I32), in_=wg_words[0].bitcast(I32))
         nc.sync.dma_start(out=xb_raw[:], in_=xb_rows)
+        nc.vector.tensor_copy(
+            out=rows[:, : 2 * W].rearrange("p (s j b i) -> p s b j i", s=2, j=PACK, i=16),
+            in_=rows_raw[:].rearrange("p (s b i j) -> p s b j i", s=2, j=PACK, i=16),
+        )
         for q in range(4):
             nc.scalar.dma_start(
                 out=planes[32 * q : 32 * q + 4, :].bitcast(I32), in_=rows[4 * q : 4 * q + 4, :].bitcast(I32)
             )
-        warm_out = new("warm_out", [16, 1], F32)
-        nc.scalar.activation(warm_out[:], rows[:, 5 * W : 5 * W + 4].bitcast(U32), SIGMOID)
         xg_codes = new("xg_codes", [P, W], I32)
         nc.sync.dma_start(out=xg_codes[:], in_=xg_words[0].rearrange("p c r -> p (c r)").bitcast(I32))
         list_b = keep.tile([P, W // 16], U16, name="list_b")
@@ -110,8 +118,6 @@ def tile_moe_combine_gated_by_token_pl_kernel(
         xa_codes = new("xa_codes", [P, 2, 2 * W], U8, tag="xb_raw")
         nc.sync.dma_start(out=xa_codes[:].bitcast(I32), in_=xa_words.rearrange("z p c -> p z c").bitcast(I32))
         nc.vector.quantize_mx(out=xb_codes[1][:].bitcast(FP8X4), scales=xb_plane[1][:], in_=xb_bf[1][:])
-        deal(wg_plane[:], planes[:, W : 2 * W], 1, 16)
-        deal(wb_plane[:], planes[:, 0:W], 1, 16)
         nc.vector.quantize_mx(out=xb_codes[0][:].bitcast(FP8X4), scales=xb_plane[0][:], in_=xb_bf[0][:])
         deal(wa_plane[:], planes[:, 2 * W : 4 * W], 2, 16)
 
@@ -141,8 +147,8 @@ def tile_moe_combine_gated_by_token_pl_kernel(
                     start=True, stop=True,
                 )
             g_banks.append(g_bank)
-            nc.scalar.copy(zb[j % 2][:, :W], bank[:])
-            nc.vector.tensor_tensor(part_b[:, j, :], zb[j % 2][:].indirect(list_b[:]), gate_b[j][:], MULT)
+            nc.scalar.copy(zb[j][:, :W], bank[:])
+            nc.vector.tensor_tensor(part_b[:, j, :], zb[j][:].indirect(list_b[:]), gate_b[j][:], MULT)
             if j == 0:
                 wa_codes = new("wa_codes", [P, 2 * W], I32, tag="gate_b0")
                 deal(wa_codes[:], wa_raw[:], 2, 4)

from contextlib import ExitStack

import concourse.mybir as mybir

F32 = mybir.dt.float32
BF16 = mybir.dt.bfloat16
I32 = mybir.dt.int32
U16 = mybir.dt.uint16
U8 = mybir.dt.uint8
FP8X4 = mybir.dt.float8_e4m3fn_x4
FP4X4 = mybir.dt.float4_e2m1fn_x4
MULT = mybir.AluOpType.mult
ADD = mybir.AluOpType.add
SIGMOID = mybir.ActivationFunctionType.Sigmoid

P = 128
PACK = 4
W = 512
SPARE = 16
CHUNKS = ((0, 256), (256, 384), (384, 512))
FLOPS = 2 * 512 * 512 * (1024 + 512 + 512)


def tile_moe_combine_gated_by_token_pl_kernel(
    tc, xa_words, xa_scales, wa_words, wa_scales, xb, wb_words, wb_scales,
    xg_words, xg_scales, wg_words, wg_scales, offs, offs2, out_0, out_1, out_2,
):
    nc = tc.nc
    with ExitStack() as ctx:
        keep = ctx.enter_context(tc.tile_pool(name="keep", bufs=1))
        psum = ctx.enter_context(tc.psum_pool(name="psum", bufs=1))

        def new(name, shape, dtype, tag=None):
            return keep.tile(shape, dtype, name=name, tag=tag or name, align_bytes=64)

        def load_rows(queue, dst, scales):
            passes = scales.shape[0]
            queue.dma_start(
                out=dst.bitcast(I32).rearrange("q (z c) -> q z c", z=passes),
                in_=scales.bitcast(I32).rearrange("z q c -> q z c"),
            )

        def deal(dst, src, passes, run):
            nc.vector.tensor_copy(
                out=dst.rearrange("p (j b i) -> p b j i", j=PACK, i=run),
                in_=src.rearrange("p (b i j) -> p b j i", j=PACK, i=run),
            )

        warm_in = new("warm_in", [P, 1], F32)
        warm_out = new("warm_out", [P, 1], F32)
        nc.vector.memset(warm_in[:], 0.0)
        nc.scalar.activation(warm_out[:], warm_in[:], SIGMOID)
        rows_raw = new("rows_raw", [P, 2 * W], U8)
        rows = new("rows", [P, 7 * W], U8)
        planes = new("planes", [P, 7 * W], U8)
        nc.gpsimd.memset(planes[:].bitcast(I32), 0)
        xg_plane, xa_plane = planes[:, 4 * W : 5 * W], planes[:, 5 * W :]
        wb_plane, wg_plane = planes[:, :W], planes[:, W : 2 * W]
        wa_plane = new("wa_plane", [P, 2 * W], U8)

        za = [new("za%d" % j, [P, W + SPARE if j < 2 else W], F32) for j in range(PACK)]
        zb = [new("zb%d" % j, [P, W + SPARE], F32) for j in range(PACK)]
        for tile in zb + za[:2]:
            nc.gpsimd.memset(tile[:, W:], 0.0)

        half = W // 2
        xb_rows = xb.rearrange("(p j) s -> p j s", j=PACK)
        xb_raw = new("xb_raw", [P, PACK, W], F32)
        wb_raw = new("wb_raw", [P, 2 * W], U8)
        for slot, scales in enumerate((wb_scales, wg_scales)):
            nc.sync.dma_start(
                out=rows_raw[:, slot * W : (slot + 1) * W].bitcast(I32),
                in_=scales.bitcast(I32).broadcast_to([P // 16, 16, W // 4]),
            )
        load_rows(nc.sync, rows[:16, 2 * W : 4 * W], wa_scales)
        load_rows(nc.sync, rows[:16, 4 * W : 5 * W], xg_scales)
        load_rows(nc.sync, rows[:16, 5 * W :], xa_scales)
        nc.sync.dma_start(out=wb_raw[:].bitcast(I32), in_=wb_words[0].bitcast(I32))
        wg_raw = new("wg_raw", [P, 2 * W], U8)
        nc.sync.dma_start(out=wg_raw[:].bitcast(I32), in_=wg_words[0].bitcast(I32))
        nc.sync.dma_start(out=xb_raw[:], in_=xb_rows)
        nc.vector.tensor_copy(
            out=rows[:, : 2 * W].rearrange("p (s j b i) -> p s b j i", s=2, j=PACK, i=16),
            in_=rows_raw[:].rearrange("p (s b i j) -> p s b j i", s=2, j=PACK, i=16),
        )
        for q in range(4):
            nc.scalar.dma_start(
                out=planes[32 * q : 32 * q + 4, :].bitcast(I32), in_=rows[4 * q : 4 * q + 4, :].bitcast(I32)
            )
        xg_codes = new("xg_codes", [P, W], I32)
        nc.sync.dma_start(out=xg_codes[:], in_=xg_words[0].rearrange("p c r -> p (c r)").bitcast(I32))
        list_b = keep.tile([P, W // 16], U16, name="list_b")
        nc.sync.dma_start(list_b[:], offs2)
        list_a = keep.tile([P, W // 16], U16, name="list_a")
        nc.sync.dma_start(list_a[:], offs)

        wb_codes = new("wb_codes", [P, 2 * W], U8)
        deal(wb_codes[:].bitcast(U16), wb_raw[:].bitcast(U16), 1, 8)
        xb_bf = [new("xb_bf%d" % h, [P, half * PACK], BF16) for h in range(2)]
        xb_codes = [new("xb_codes%d" % h, [P, half], I32) for h in range(2)]
        xb_plane = [new("xb_plane%d" % h, [P, half], U8) for h in range(2)]

        def weave(engine_copy, dst, src):
            engine_copy(
                out=dst.rearrange("p (c i t) -> p c t i", i=4, t=PACK),
                in_=src.rearrange("p t (c i) -> p c t i", i=4),
            )

        wg_codes = new("wg_codes", [P, 2 * W], U8)
        deal(wg_codes[:].bitcast(U16), wg_raw[:].bitcast(U16), 1, 8)
        wa_raw = new("wa_raw", [P, 2 * W], I32, tag="wg_raw")
        nc.sync.dma_start(
            out=wa_raw[:].rearrange("p (z c) -> p z c", z=2),
            in_=wa_words.rearrange("z p c r -> p z (c r)").bitcast(I32),
        )
        weave(nc.scalar.copy, xb_bf[0][:], xb_raw[:, :, :half])
        weave(nc.vector.tensor_copy, xb_bf[1][:], xb_raw[:, :, half:])
        xa_codes = new("xa_codes", [P, 2, 2 * W], U8, tag="xb_raw")
        nc.sync.dma_start(out=xa_codes[:].bitcast(I32), in_=xa_words.rearrange("z p c -> p z c").bitcast(I32))
        nc.vector.quantize_mx(out=xb_codes[1][:].bitcast(FP8X4), scales=xb_plane[1][:], in_=xb_bf[1][:])
        nc.vector.quantize_mx(out=xb_codes[0][:].bitcast(FP8X4), scales=xb_plane[0][:], in_=xb_bf[0][:])
        deal(wa_plane[:], planes[:, 2 * W : 4 * W], 2, 16)

        gate_b = [new("gate_b%d" % j, [P, W], F32) for j in range(PACK)]
        gate_a = gate_b[1:] + [new("gate_a3", [P, W], F32)]
        part_b = new("part_b", [P, PACK, W], F32)
        g_banks = []
        for j in range(PACK):
            g_bank = psum.tile([P, W], F32, name="g_bank%d" % j, tag="bank%d" % j)
            nc.tensor.matmul_mx(
                out=g_bank[:],
                lhsT=wg_codes[:, 2 * P * j : 2 * P * (j + 1)].bitcast(FP4X4),
                lhsT_scale=wg_plane[:, P * j : P * (j + 1)],
                rhs=xg_codes[:].bitcast(FP8X4),
                rhs_scale=xg_plane,
                start=True, stop=True,
            )
            nc.scalar.activation(gate_b[j][:], g_bank[:], SIGMOID, scale=-1.0)
            bank = psum.tile([P, W], F32, name="zb_bank%d" % j, tag="bank%d" % (j + 1))
            for h in (1, 0):
                nc.tensor.matmul_mx(
                    out=bank[:, h * half : (h + 1) * half],
                    lhsT=wb_codes[:, 2 * P * j : 2 * P * (j + 1)].bitcast(FP4X4),
                    lhsT_scale=wb_plane[:, P * j : P * (j + 1)],
                    rhs=xb_codes[h][:].bitcast(FP8X4),
                    rhs_scale=xb_plane[h][:],
                    start=True, stop=True,
                )
            g_banks.append(g_bank)
            nc.scalar.copy(zb[j][:, :W], bank[:])
            nc.vector.tensor_tensor(part_b[:, j, :], zb[j][:].indirect(list_b[:]), gate_b[j][:], MULT)
            if j == 0:
                wa_codes = new("wa_codes", [P, 2 * W], I32, tag="gate_b0")
                deal(wa_codes[:], wa_raw[:], 2, 4)

        for j in range(PACK):
            bank = psum.tile([P, W], F32, name="za_bank%d" % j, tag="bank%d" % (PACK + (j + 1) % PACK))
            for z in range(2):
                cols = slice(2 * P * j + P * z, 2 * P * j + P * (z + 1))
                nc.tensor.matmul_mx(
                    out=bank[:],
                    lhsT=wa_codes[:, cols].bitcast(FP8X4),
                    lhsT_scale=wa_plane[:, cols],
                    rhs=xa_codes[:, z, :].bitcast(FP4X4),
                    rhs_scale=xa_plane[:, z * W : (z + 1) * W],
                    start=(z == 0), stop=(z == 1),
                )
            nc.scalar.copy(za[j][:, :W], bank[:])
            first = W if j < 2 else half
            nc.scalar.activation(gate_a[j][:, :first], g_banks[j][:, :first], SIGMOID)
        for j in (2, 3):
            nc.scalar.activation(gate_a[j][:, half:], g_banks[j][:, half:], SIGMOID)

        part_a = new("part_a", [P, PACK, W], F32)
        for j in range(2):
            nc.vector.tensor_tensor(part_a[:, j, :], za[j][:].indirect(list_a[:]), gate_a[j][:], MULT)

        y_rows = out_0.rearrange("(p j) t -> p j t", j=PACK)
        words_out = out_1[0].rearrange("p c r -> p (c r)").bitcast(I32)
        y_plane = new("y_plane", [P, W], U8)

        def gather(c, j):
            t0, t1 = CHUNKS[c]
            nc.vector.tensor_tensor(
                part_a[:, j, t0:t1], za[j][:].indirect(list_a[:, t0 // 16 : t1 // 16]), gate_a[j][:, t0:t1], MULT
            )

        ys = {}
        ybf = {}

        def add(c):
            t0, t1 = CHUNKS[c]
            ys[c] = new("y%d" % c, [P, PACK, t1 - t0], F32)
            nc.vector.tensor_tensor(ys[c][:], part_a[:, :, t0:t1], part_b[:, :, t0:t1], ADD)
            nc.sync.dma_start(out=y_rows[:, :, t0:t1], in_=ys[c][:])

        def round_(c, engine_copy):
            t0, t1 = CHUNKS[c]
            ybf[c] = new("ybf%d" % c, [P, (t1 - t0) * PACK], BF16)
            weave(engine_copy, ybf[c][:], ys[c][:])

        y_codes = new("y_codes", [P, W], I32)

        def quant(c):
            t0, t1 = CHUNKS[c]
            nc.vector.quantize_mx(out=y_codes[:, t0:t1].bitcast(FP8X4), scales=y_plane[:, t0:t1], in_=ybf[c][:])

        gather(0, 2)
        gather(0, 3)
        gather(1, 2)
        add(0)
        round_(0, nc.scalar.copy)
        gather(1, 3)
        gather(2, 2)
        add(1)
        round_(1, nc.scalar.copy)
        gather(2, 3)
        quant(0)
        nc.sync.dma_start(out=words_out[:, :half], in_=y_codes[:, :half])
        add(2)
        quant(1)
        round_(2, nc.vector.tensor_copy)
        quant(2)
        nc.sync.dma_start(out=words_out[:, half:], in_=y_codes[:, half:])
        for q in range(4):
            nc.scalar.dma_start(
                out=out_2[0, 4 * q : 4 * q + 4, :].bitcast(I32), in_=y_plane[32 * q : 32 * q + 4, :].bitcast(I32)
            )
